import numpy as np
import ml_dtypes


def mxq(x, axis, fmt="e4m3"):
    dtype, down = {"e4m3": (ml_dtypes.float8_e4m3fn, 7), "e5m2": (ml_dtypes.float8_e5m2, 14)}[fmt]
    v = np.moveaxis(np.asarray(x, np.float32).astype(ml_dtypes.bfloat16).astype(np.float64), axis, -1)
    blocks = v.reshape(v.shape[:-1] + (-1, 32))
    amax = np.abs(blocks).max(-1, keepdims=True)
    byte = np.maximum(np.where(amax > 0, np.frexp(amax)[1] - 1 + 127, 0) - down, 1)
    scale = np.exp2(byte - 127.0)
    codes = (blocks / scale).astype(np.float32).astype(dtype).astype(np.float64)
    return np.moveaxis((codes * scale).reshape(v.shape), -1, axis)


WIDE = False


def mx_kscale(k):
    if not WIDE:
        return np.ones(k)
    levels = np.array([10, -10, 5, -5, 0])
    if k % 512:
        return np.exp2(np.random.permutation(np.resize(levels, k // 32))).repeat(32)
    a = np.empty((k // 512, 16))
    for p in range(k // 512):
        a[p, :8] = np.random.permutation(np.resize(levels, 8))
        for g in range(8):
            far = levels[np.abs(levels - a[p, g]) >= 10]
            a[p, g + 8] = far[np.random.randint(len(far))]
    return np.exp2(a.ravel()).repeat(32)


def f64(x):
    return np.asarray(x).astype(np.float64)


def striped(idx):
    return np.tile(idx.reshape(-1, 16).T, (8, 1)).astype(np.uint16)


def unstriped(offs):
    return offs[:16].T.reshape(-1).astype(np.int64)


def pack_weight(w):
    k, n = w.shape
    w = f64(np.asarray(w, np.float32).astype(ml_dtypes.bfloat16)).reshape(k // 32, 32, n)
    amax = np.abs(w).max(1)
    byte = np.clip(np.where(amax > 0, np.frexp(amax)[1] - 1 + 127 - 7, 1), 1, 254)
    scaled = (w * np.exp2(127.0 - byte)[:, None, :]).reshape(k, n).astype(np.float32)
    words = np.ascontiguousarray(scaled.reshape(k // 512, 128, 4, n).transpose(0, 1, 3, 2)).astype(ml_dtypes.float8_e4m3fn).view(np.uint8)
    return words, np.ascontiguousarray(byte.astype(np.uint8).reshape(k // 512, 16, n))


def unpack_weight(words, scales):
    g, p, n, _ = words.shape
    vals = np.ascontiguousarray(words).view(ml_dtypes.float8_e4m3fn).astype(np.float64) * np.repeat(np.exp2(scales.astype(np.float64) - 127.0), 8, axis=1)[..., None]
    return vals.transpose(0, 1, 3, 2).reshape(g * 512, n)


def sigmoid(v):
    return 1.0 / (1.0 + np.exp(-np.maximum(v, -700.0)))


K, T, S, D, H, Z, W = 512, 2048, 512, 2, 512, 512, 2048
P = 2 ** 7


def setup_inputs():
    n = np.random.standard_normal
    s = mx_kscale(K)[:, None]
    packed_xT = pack_weight(n((K, T)) * s)
    packed_eT = pack_weight(n((K, W)) * s)
    return {
        "x_words": packed_xT[0],
        "x_scales": packed_xT[1],
        "w1": (n((K, H)) / np.sqrt(K) / s).astype(np.float32),
        "w2": (n((K, H)) / np.sqrt(K) / s).astype(np.float32),
        "e_words": packed_eT[0],
        "e_scales": packed_eT[1],
        "unit": (np.random.uniform(0.6, 1.4, (K, 1)) / np.sqrt(K) / s).astype(np.float32),
        "thr": (np.tile(np.random.uniform(-0.3, 0.6, W), (P, 1))).astype(np.float32),
        "expr": (np.tile(np.random.uniform(0.3, 1.5, W), (P, 1))).astype(np.float32),
        "offs": striped(np.random.permutation(T)[:S]),
        "fl": striped(np.random.permutation(S)),
        "all_": striped(np.random.permutation(W)[:Z]),
    }


def reference(x_words, x_scales, w1, w2, e_words, e_scales, unit, thr, expr, offs, fl, all_):
    xq = unpack_weight(x_words, x_scales)[:, unstriped(offs)]
    y = mxq(f64(w1), 0, "e4m3").T @ xq
    ya = mxq(f64(w2), 0, "e4m3").T @ xq
    af = ya[:, unstriped(fl)]
    ctx = y * (0.8 * sigmoid(af) + 0.4)
    pep = ctx.reshape(len(ctx), -1, D).sum(axis=2)
    absa = np.abs(ya)
    pq = pep + 0.3 * (absa.reshape(len(absa), -1, D).max(axis=2))
    hid = f64(unit) * pq
    e_all_ = unpack_weight(e_words, e_scales)[:, unstriped(all_)]
    sc = mxq(hid, 0, "e4m3").T @ e_all_
    mg = sc - (f64(thr)[:1][:, unstriped(all_)])
    bind = sigmoid(2.5 * mg)
    return np.log(-1.0 * (0.8 * bind) + 1.0 + 0.1) + 0.5 * (f64(expr)[:1][:, unstriped(all_)])

@@ -1,0 +1,238 @@
+from contextlib import ExitStack
+
+import concourse.mybir as mybir
+from concourse.masks import make_identity
+
+F32 = mybir.dt.float32
+BF16 = mybir.dt.bfloat16
+I32 = mybir.dt.int32
+U32 = mybir.dt.uint32
+U16 = mybir.dt.uint16
+U8 = mybir.dt.uint8
+FP8X4 = mybir.dt.float8_e4m3fn_x4
+ACT = mybir.ActivationFunctionType
+ALU = mybir.AluOpType
+
+P = 128
+K, T, S, H, Z, V = 512, 2048, 512, 512, 512, 256
+PACK = 4
+FLOPS = 2 * K * H * S * 2 + 2 * H * V * Z
+
+
+def tile_picked_yhlaepi_esc_p_kernel(
+    tc, x_words, x_scales, w1, w2, e_words, e_scales, unit, thr, expr, offs, fl, all_, out
+):
+    nc = tc.nc
+    with ExitStack() as ctx:
+        lists = ctx.enter_context(tc.tile_pool(name="lists", bufs=1))
+        sb = ctx.enter_context(tc.tile_pool(name="sb", bufs=1))
+        psum = ctx.enter_context(tc.psum_pool(name="psum", bufs=1))
+
+        def bank(n, name):
+            return psum.tile([P, 512], F32, name=name, tag="bank%d" % n)
+
+        offs_t = lists.tile([P, S // 16], U16, name="offs_t")
+        fl_t = lists.tile([P, S // 16], U16, name="fl_t")
+        all_t = lists.tile([P, Z // 16], U16, name="all_t")
+
+        xw = sb.tile([P, T], I32, name="xw", tag="x_then_w1", align_bytes=64)
+        xs = sb.tile([P, T], U8, name="xs", tag="chain0", align_bytes=64)
+        es = sb.tile([P, T], U8, name="es", align_bytes=64)
+        te = sb.tile([P, T], F32, name="te", tag="chain1", align_bytes=64)
+        w2_raw = sb.tile([P, PACK, H], F32, name="w2_raw", tag="w2_then_e", align_bytes=64)
+        unit_t = sb.tile([P, PACK], F32, name="unit_t", align_bytes=64)
+
+        def load_scales(queue, tile, scales):
+            for q in range(4):
+                queue.dma_start(
+                    out=tile[32 * q : 32 * q + 4, :].bitcast(I32), in_=scales[0][4 * q : 4 * q + 4, :].bitcast(I32)
+                )
+
+        def words(ap):
+            return ap[0].rearrange("p n t -> p (n t)").bitcast(I32)
+
+        nc.gpsimd.memset(xs[:].bitcast(I32), 0)
+        nc.sync.dma_start(offs_t[:], offs)
+        nc.sync.dma_start(all_t[:], all_)
+        nc.sync.dma_start(fl_t[:], fl)
+        nc.sync.dma_start(out=xw[:], in_=words(x_words))
+        nc.sync.dma_start(out=w2_raw[:], in_=w2.rearrange("(p j) c -> p j c", j=PACK))
+        load_scales(nc.scalar, xs, x_scales)
+        nc.vector.memset(te[:], 0.0)
+        nc.gpsimd.memset(es[:].bitcast(I32), 0)
+        nc.scalar.dma_start(out=te[0:1, :], in_=thr[0:1, :])
+        nc.scalar.dma_start(out=te[1:2, :], in_=expr[0:1, :])
+        load_scales(nc.gpsimd, es, e_scales)
+        nc.gpsimd.dma_start(out=unit_t[:], in_=unit.rearrange("(p t) o -> p (t o)", t=PACK))
+        ident = sb.tile([P, P], F32, name="ident", align_bytes=64)
+        make_identity(nc, ident[:])
+
+        xg = sb.tile([P, S], U32, name="xg", align_bytes=64)
+        xsg = sb.tile([P, S], U8, name="xsg", align_bytes=64)
+        eg = sb.tile([P, Z], U32, name="eg", align_bytes=64)
+        teg = sb.tile([P, Z], F32, name="teg", align_bytes=64)
+
+        def weight_tiles(name, tag):
+            return [
+                (
+                    sb.tile([P, 2 * P * PACK], BF16, name="%s_bf%d" % (name, u), tag="%s%d" % (tag, u), align_bytes=64),
+                    sb.tile([P, 2 * P], U32, name="%s_q%d" % (name, u), align_bytes=64),
+                    sb.tile([P, 2 * P], U8, name="%s_s%d" % (name, u), align_bytes=64),
+                )
+                for u in range(2)
+            ]
+
+
+        def deal(copy, tiles, raw, u):
+            copy(
+                tiles[u][0][:].rearrange("p (t m j) -> p m j t", t=2, j=PACK),
+                raw[:].rearrange("p j (m t) -> p m j t", t=PACK)[:, :, :, 2 * u : 2 * u + 2],
+            )
+
+        def quantise_weight(tiles, u):
+            nc.vector.quantize_mx(out=tiles[u][1][:].bitcast(FP8X4), scales=tiles[u][2][:], in_=tiles[u][0][:])
+
+        nc.vector.tensor_copy(xg[:], xw[:].bitcast(U32).indirect(offs_t[:]))
+        nc.vector.tensor_copy(xsg[:], xs[:].indirect(offs_t[:]))
+        w1_raw = sb.tile([P, PACK, H], F32, name="w1_raw", tag="x_then_w1", align_bytes=64)
+        nc.sync.dma_start(out=w1_raw[:], in_=w1.rearrange("(p j) c -> p j c", j=PACK))
+        nc.scalar.activation(teg[:], te[:].indirect(all_t[:]), ACT.Copy)
+        w2_t = weight_tiles("w2", "chain")
+        w1_t = weight_tiles("w1", "w1_bf")
+        deal(nc.vector.tensor_copy, w2_t, w2_raw, 0)
+        deal(nc.scalar.copy, w2_t, w2_raw, 1)
+        ew = sb.tile([P, T], I32, name="ew", tag="w2_then_e", align_bytes=64)
+        nc.sync.dma_start(out=ew[:], in_=words(e_words))
+        quantise_weight(w2_t, 0)
+        quantise_weight(w2_t, 1)
+
+        def first_product(tiles, first_bank, name):
+            banks = []
+            for t in range(PACK):
+                b = bank(first_bank + t, "%s%d" % (name, t))
+                cols = slice((t % 2) * P, (t % 2 + 1) * P)
+                nc.tensor.matmul_mx(
+                    out=b[:], lhsT=tiles[t // 2][1][:, cols].bitcast(FP8X4), lhsT_scale=tiles[t // 2][2][:, cols],
+                    rhs=xg[:].bitcast(FP8X4), rhs_scale=xsg[:], start=True, stop=True,
+                )
+                banks.append(b)
+            return banks
+
+        ya = first_product(w2_t, 0, "ya")
+
+        te_ps = bank(7, "te_ps")
+        for c in range(4):
+            nc.tensor.transpose(te_ps[:, c * P : (c + 1) * P], teg[:, c * P : (c + 1) * P], ident[:])
+
+        sig = [sb.tile([P, S], F32, name="sig%d" % t, align_bytes=64) for t in range(PACK)]
+        for t in range(PACK):
+            nc.scalar.activation(sig[t][:], ya[t][:], ACT.Sigmoid)
+
+        te_col = sb.tile([P, 4, 2], F32, name="te_col", align_bytes=64)
+        thr_col = sb.tile([P, 4], F32, name="thr_col", tag="thr_then_logs", align_bytes=64)
+        nc.scalar.copy(te_col[:], te_ps[:].rearrange("p (c r) -> p c r", r=P)[:, :, 0:2])
+        nc.vector.tensor_scalar(thr_col[:], te_col[:, :, 0], -2.5, None, ALU.mult)
+
+        esg = sb.tile([P, Z], U8, name="esg", tag="chain1", align_bytes=64)
+        nc.vector.tensor_copy(esg[:], es[:].indirect(all_t[:]))
+        u8 = sb.tile([P, PACK], F32, name="u8", align_bytes=64)
+        u3 = sb.tile([P, PACK], F32, name="u3", align_bytes=64)
+        nc.vector.tensor_scalar(u8[:], unit_t[:], 0.8, None, ALU.mult)
+        nc.vector.tensor_scalar(u3[:], unit_t[:], 0.3, None, ALU.mult)
+        for u in range(2):
+            deal(nc.vector.tensor_copy, w1_t, w1_raw, u)
+        for u in range(2):
+            quantise_weight(w1_t, u)
+        y = first_product(w1_t, 4, "y")
+        nc.vector.tensor_copy(eg[:], ew[:].bitcast(U32).indirect(all_t[:]))
+
+        mag = [sb.tile([P, S], F32, name="mag%d" % t, align_bytes=64) for t in range(PACK)]
+        big = [sb.tile([P, V], F32, name="big%d" % t, align_bytes=64) for t in range(PACK)]
+
+        HS = S // 2
+        HV = V // 2
+        gate = [[sb.tile([P, HS], F32, name="gate%d_%d" % (h, t), align_bytes=64) for t in range(PACK)] for h in range(2)]
+        ctx_t = [sb.tile([P, PACK * HS], F32, name="ctx%d" % h, align_bytes=64) for h in range(2)]
+        part = [sb.tile([P, PACK * HV], F32, name="part%d" % h, align_bytes=64) for h in range(2)]
+        hid_bf = [sb.tile([P, PACK * HV], BF16, name="hid_bf%d" % h, align_bytes=64) for h in range(2)]
+        hid_q = [sb.tile([P, HV], U32, name="hid_q%d" % h, align_bytes=64) for h in range(2)]
+        hid_s = [sb.tile([P, HV], U8, name="hid_s%d" % h, align_bytes=64) for h in range(2)]
+        bind = [sb.tile([P, 4 * HV], F32, name="bind%d" % h, align_bytes=64) for h in range(2)]
+
+        def magnitude(t):
+            nc.scalar.activation(mag[t][:], ya[t][:], ACT.Abs)
+            nc.vector.tensor_tensor(big[t][:], mag[t][:, 0::2], mag[t][:, 1::2], ALU.max)
+
+        def modulate(h, t):
+            nc.scalar.activation(
+                gate[h][t][:], sig[t][:].indirect(fl_t[:, h * (HS // 16) : (h + 1) * (HS // 16)]), ACT.Copy, bias=0.5
+            )
+            nc.vector.scalar_tensor_tensor(
+                ctx_t[h][:, t * HS : (t + 1) * HS], gate[h][t][:], u8[:, t : t + 1], y[t][:, h * HS : (h + 1) * HS],
+                ALU.mult, ALU.mult,
+            )
+
+        def join(h, t):
+            nc.vector.scalar_tensor_tensor(
+                part[h][:, t * HV : (t + 1) * HV], big[t][:, h * HV : (h + 1) * HV], u3[:, t : t + 1],
+                ctx_t[h][:, t * HS : (t + 1) * HS : 2], ALU.mult, ALU.add,
+            )
+
+        def quantise(h):
+            nc.vector.tensor_tensor(
+                hid_bf[h][:].rearrange("p (c i t) -> p c t i", i=4, t=PACK),
+                part[h][:].rearrange("p (t c i) -> p c t i", i=4, t=PACK),
+                ctx_t[h][:].rearrange("p (t c i d) -> p c t i d", i=4, t=PACK, d=2)[:, :, :, :, 1],
+                ALU.add,
+            )
+            nc.vector.quantize_mx(out=hid_q[h][:].bitcast(FP8X4), scales=hid_s[h][:], in_=hid_bf[h][:])
+
+        def score(h):
+            b = bank(h, "sc%d" % h)
+            for c in range(4):
+                nc.tensor.matmul_mx(
+                    out=b[:, c * HV : (c + 1) * HV], lhsT=eg[:, c * P : (c + 1) * P].bitcast(FP8X4),
+                    lhsT_scale=esg[:, c * P : (c + 1) * P], rhs=hid_q[h][:].bitcast(FP8X4), rhs_scale=hid_s[h][:],
+                    start=True, stop=True,
+                )
+            for c in range(4):
+                nc.scalar.activation(
+                    bind[h][:, c * HV : (c + 1) * HV], b[:, c * HV : (c + 1) * HV], ACT.Sigmoid,
+                    bias=thr_col[:, c : c + 1], scale=2.5,
+                )
+
+        for t in range(PACK):
+            magnitude(t)
+            modulate(0, t)
+            if t > 0:
+                join(0, t - 1)
+        modulate(1, 0)
+        join(0, PACK - 1)
+        modulate(1, 1)
+        quantise(0)
+        join(1, 0)
+        modulate(1, 2)
+        join(1, 1)
+        modulate(1, 3)
+        join(1, 2)
+        join(1, 3)
+        score(0)
+        quantise(1)
+
+        expr_ps = bank(2, "expr_ps")
+        for c in range(4):
+            nc.tensor.transpose(expr_ps[:, c * P : (c + 1) * P], te_col[:, c, 1:2].to_broadcast([P, P]), ident[:])
+        score(1)
+
+        logs = sb.tile([P, 2 * Z], F32, name="logs", tag="thr_then_logs", align_bytes=64)
+        for h in range(2):
+            turned = bank(4 + h, "turned%d" % h)
+            for c in range(4):
+                nc.tensor.transpose(turned[:, c * P : (c + 1) * P], bind[h][:, c * HV : (c + 1) * HV], ident[:])
+            for half in range(2):
+                cols = slice(half * 256, (half + 1) * 256)
+                piece = logs[:, h * Z + half * 256 : h * Z + (half + 1) * 256]
+                res = sb.tile([P, 256], F32, name="res%d_%d" % (h, half), align_bytes=64)
+                nc.scalar.activation(piece, turned[:, cols], ACT.Ln, bias=1.1, scale=-0.8)
+                nc.vector.scalar_tensor_tensor(res[:], expr_ps[:, cols], 0.5, piece, ALU.mult, ALU.add)
+                nc.sync.dma_start(out=out[h * P : (h + 1) * P, cols], in_=res[:])

@@ -16,6 +16,8 @@ ALU = mybir.AluOpType
 P = 128
 K, T, S, H, Z, V = 512, 2048, 512, 512, 512, 256
 PACK = 4
+HS = S // 2
+HV = V // 2
 FLOPS = 2 * K * H * S * 2 + 2 * H * V * Z
 
 
@@ -31,133 +33,133 @@ def tile_picked_yhlaepi_esc_p_kernel(
         def bank(n, name):
             return psum.tile([P, 512], F32, name=name, tag="bank%d" % n)
 
+        def tile(name, columns, dtype, tag=None):
+            return sb.tile([P, columns], dtype, name=name, tag=tag or name, align_bytes=64)
+
         offs_t = lists.tile([P, S // 16], U16, name="offs_t")
         fl_t = lists.tile([P, S // 16], U16, name="fl_t")
         all_t = lists.tile([P, Z // 16], U16, name="all_t")
 
-        xw = sb.tile([P, T], I32, name="xw", tag="x_then_w1", align_bytes=64)
-        xs = sb.tile([P, T], U8, name="xs", tag="chain0", align_bytes=64)
-        es = sb.tile([P, T], U8, name="es", align_bytes=64)
-        te = sb.tile([P, T], F32, name="te", tag="chain1", align_bytes=64)
-        w2_raw = sb.tile([P, PACK, H], F32, name="w2_raw", tag="w2_then_e", align_bytes=64)
-        unit_t = sb.tile([P, PACK], F32, name="unit_t", align_bytes=64)
+        xw = tile("xw", T, I32)
+        xs = tile("xs", T, U8)
+        es = tile("es", T, U8)
+        te = tile("te", T, F32)
+        w2_raw = tile("w2_raw", PACK * H, F32)
+        w1_raw = tile("w1_raw", PACK * H, F32)
+        unit_t = tile("unit_t", PACK, F32)
+        ident = tile("ident", P, F32)
 
-        def load_scales(queue, tile, scales):
+        def load_scales(queue, dst, scales):
             for q in range(4):
                 queue.dma_start(
-                    out=tile[32 * q : 32 * q + 4, :].bitcast(I32), in_=scales[0][4 * q : 4 * q + 4, :].bitcast(I32)
+                    out=dst[32 * q : 32 * q + 4, :].bitcast(I32), in_=scales[0][4 * q : 4 * q + 4, :].bitcast(I32)
                 )
 
-        def words(ap):
-            return ap[0].rearrange("p n t -> p (n t)").bitcast(I32)
+        def load_words(dst, words):
+            nc.sync.dma_start(out=dst[:], in_=words[0].rearrange("p n t -> p (n t)").bitcast(I32))
+
+        def load_weight(dst, w):
+            nc.sync.dma_start(out=dst[:], in_=w.rearrange("(p j) c -> p (j c)", j=PACK))
 
         nc.gpsimd.memset(xs[:].bitcast(I32), 0)
+        warm = tile("warm", 2, F32)
+        nc.vector.memset(warm[:, 0:1], 0.0)
+        nc.scalar.activation(warm[:, 1:2], warm[:, 0:1], ACT.Sigmoid)
+        nc.vector.memset(te[:, : T // 2], 0.0)
+        nc.gpsimd.memset(te[:, T // 2 :], 0.0)
+        nc.vector.memset(es[:].bitcast(I32), 0)
+        make_identity(nc, ident[:])
+
         nc.sync.dma_start(offs_t[:], offs)
         nc.sync.dma_start(all_t[:], all_)
         nc.sync.dma_start(fl_t[:], fl)
-        nc.sync.dma_start(out=xw[:], in_=words(x_words))
-        nc.sync.dma_start(out=w2_raw[:], in_=w2.rearrange("(p j) c -> p j c", j=PACK))
-        load_scales(nc.scalar, xs, x_scales)
-        nc.vector.memset(te[:], 0.0)
-        nc.gpsimd.memset(es[:].bitcast(I32), 0)
-        nc.scalar.dma_start(out=te[0:1, :], in_=thr[0:1, :])
-        nc.scalar.dma_start(out=te[1:2, :], in_=expr[0:1, :])
-        load_scales(nc.gpsimd, es, e_scales)
-        nc.gpsimd.dma_start(out=unit_t[:], in_=unit.rearrange("(p t) o -> p (t o)", t=PACK))
-        ident = sb.tile([P, P], F32, name="ident", align_bytes=64)
-        make_identity(nc, ident[:])
+        load_weight(w2_raw, w2)
+        load_scales(nc.sync, xs, x_scales)
+        nc.sync.dma_start(out=te[0:1, :], in_=thr[0:1, :])
+        nc.sync.dma_start(out=te[1:2, :], in_=expr[0:1, :])
+        load_words(xw, x_words)
+        nc.sync.dma_start(out=unit_t[:], in_=unit.rearrange("(p t) o -> p (t o)", t=PACK))
+        load_scales(nc.sync, es, e_scales)
+        load_weight(w1_raw, w1)
 
-        xg = sb.tile([P, S], U32, name="xg", align_bytes=64)
-        xsg = sb.tile([P, S], U8, name="xsg", align_bytes=64)
-        eg = sb.tile([P, Z], U32, name="eg", align_bytes=64)
-        teg = sb.tile([P, Z], F32, name="teg", align_bytes=64)
-
-        def weight_tiles(name, tag):
+        def weight_tiles(name):
             return [
-                (
-                    sb.tile([P, 2 * P * PACK], BF16, name="%s_bf%d" % (name, u), tag="%s%d" % (tag, u), align_bytes=64),
-                    sb.tile([P, 2 * P], U32, name="%s_q%d" % (name, u), align_bytes=64),
-                    sb.tile([P, 2 * P], U8, name="%s_s%d" % (name, u), align_bytes=64),
-                )
+                (tile("%s_bf%d" % (name, u), 2 * P * PACK, BF16), tile("%s_q%d" % (name, u), 2 * P, U32),
+                 tile("%s_s%d" % (name, u), 2 * P, U8))
                 for u in range(2)
             ]
-
 
         def deal(copy, tiles, raw, u):
             copy(
                 tiles[u][0][:].rearrange("p (t m j) -> p m j t", t=2, j=PACK),
-                raw[:].rearrange("p j (m t) -> p m j t", t=PACK)[:, :, :, 2 * u : 2 * u + 2],
+                raw[:].rearrange("p (j m t) -> p m j t", t=PACK, j=PACK)[:, :, :, 2 * u : 2 * u + 2],
             )
 
         def quantise_weight(tiles, u):
             nc.vector.quantize_mx(out=tiles[u][1][:].bitcast(FP8X4), scales=tiles[u][2][:], in_=tiles[u][0][:])
 
-        nc.vector.tensor_copy(xg[:], xw[:].bitcast(U32).indirect(offs_t[:]))
-        nc.vector.tensor_copy(xsg[:], xs[:].indirect(offs_t[:]))
-        w1_raw = sb.tile([P, PACK, H], F32, name="w1_raw", tag="x_then_w1", align_bytes=64)
-        nc.sync.dma_start(out=w1_raw[:], in_=w1.rearrange("(p j) c -> p j c", j=PACK))
-        nc.scalar.activation(teg[:], te[:].indirect(all_t[:]), ACT.Copy)
-        w2_t = weight_tiles("w2", "chain")
-        w1_t = weight_tiles("w1", "w1_bf")
+        xsg = tile("xsg", S, U8)
+        xg = tile("xg", S, U32)
+        teg = tile("teg", Z, F32)
+        w2_t = weight_tiles("w2")
+        w1_t = weight_tiles("w1")
+
         deal(nc.vector.tensor_copy, w2_t, w2_raw, 0)
         deal(nc.scalar.copy, w2_t, w2_raw, 1)
-        ew = sb.tile([P, T], I32, name="ew", tag="w2_then_e", align_bytes=64)
-        nc.sync.dma_start(out=ew[:], in_=words(e_words))
-        quantise_weight(w2_t, 0)
-        quantise_weight(w2_t, 1)
+        nc.vector.tensor_copy(xsg[:], xs[:].indirect(offs_t[:]))
+        ew = tile("ew", T, I32, tag="w2_raw")
+        load_words(ew, e_words)
+        for u in range(2):
+            quantise_weight(w2_t, u)
+        nc.vector.tensor_copy(xg[:], xw[:].bitcast(U32).indirect(offs_t[:]))
+        esg = tile("esg", Z, U8, tag="xw")
+        nc.vector.tensor_copy(esg[:], es[:].indirect(all_t[:]))
+        nc.scalar.activation(teg[:], te[:].indirect(all_t[:]), ACT.Copy)
 
-        def first_product(tiles, first_bank, name):
-            banks = []
-            for t in range(PACK):
-                b = bank(first_bank + t, "%s%d" % (name, t))
-                cols = slice((t % 2) * P, (t % 2 + 1) * P)
-                nc.tensor.matmul_mx(
-                    out=b[:], lhsT=tiles[t // 2][1][:, cols].bitcast(FP8X4), lhsT_scale=tiles[t // 2][2][:, cols],
-                    rhs=xg[:].bitcast(FP8X4), rhs_scale=xsg[:], start=True, stop=True,
-                )
-                banks.append(b)
-            return banks
+        def product(tiles, t, n, name):
+            b = bank(n, "%s%d" % (name, t))
+            cols = slice((t % 2) * P, (t % 2 + 1) * P)
+            nc.tensor.matmul_mx(
+                out=b[:], lhsT=tiles[t // 2][1][:, cols].bitcast(FP8X4), lhsT_scale=tiles[t // 2][2][:, cols],
+                rhs=xg[:].bitcast(FP8X4), rhs_scale=xsg[:], start=True, stop=True,
+            )
+            return b
 
-        ya = first_product(w2_t, 0, "ya")
+        ya = [product(w2_t, t, t, "ya") for t in range(PACK)]
 
         te_ps = bank(7, "te_ps")
         for c in range(4):
             nc.tensor.transpose(te_ps[:, c * P : (c + 1) * P], teg[:, c * P : (c + 1) * P], ident[:])
 
-        sig = [sb.tile([P, S], F32, name="sig%d" % t, align_bytes=64) for t in range(PACK)]
+        sig = [tile("sig%d" % t, S, F32) for t in range(PACK)]
         for t in range(PACK):
             nc.scalar.activation(sig[t][:], ya[t][:], ACT.Sigmoid)
-
-        te_col = sb.tile([P, 4, 2], F32, name="te_col", align_bytes=64)
-        thr_col = sb.tile([P, 4], F32, name="thr_col", tag="thr_then_logs", align_bytes=64)
-        nc.scalar.copy(te_col[:], te_ps[:].rearrange("p (c r) -> p c r", r=P)[:, :, 0:2])
-        nc.vector.tensor_scalar(thr_col[:], te_col[:, :, 0], -2.5, None, ALU.mult)
-
-        esg = sb.tile([P, Z], U8, name="esg", tag="chain1", align_bytes=64)
-        nc.vector.tensor_copy(esg[:], es[:].indirect(all_t[:]))
-        u8 = sb.tile([P, PACK], F32, name="u8", align_bytes=64)
-        u3 = sb.tile([P, PACK], F32, name="u3", align_bytes=64)
-        nc.vector.tensor_scalar(u8[:], unit_t[:], 0.8, None, ALU.mult)
-        nc.vector.tensor_scalar(u3[:], unit_t[:], 0.3, None, ALU.mult)
         for u in range(2):
             deal(nc.vector.tensor_copy, w1_t, w1_raw, u)
+
+        te_col = tile("te_col", 8, F32)
+        thr_col = tile("thr_col", 4, F32, tag="thr_then_logs")
+        nc.scalar.copy(te_col[:].rearrange("p (c r) -> p c r", r=2), te_ps[:].rearrange("p (c r) -> p c r", r=P)[:, :, 0:2])
+        u8 = tile("u8", PACK, F32)
+        u3 = tile("u3", PACK, F32)
+        nc.gpsimd.tensor_scalar(u8[:], unit_t[:], 0.8, 0.0, ALU.mult, ALU.add)
+        nc.gpsimd.tensor_scalar(u3[:], unit_t[:], 0.3, 0.0, ALU.mult, ALU.add)
+        nc.gpsimd.tensor_scalar(thr_col[:], te_col[:, 0::2], -2.5, 0.0, ALU.mult, ALU.add)
+
+        y = []
         for u in range(2):
             quantise_weight(w1_t, u)
-        y = first_product(w1_t, 4, "y")
-        nc.vector.tensor_copy(eg[:], ew[:].bitcast(U32).indirect(all_t[:]))
+            y.extend(product(w1_t, t, 4 + t, "y") for t in (2 * u, 2 * u + 1))
 
-        mag = [sb.tile([P, S], F32, name="mag%d" % t, align_bytes=64) for t in range(PACK)]
-        big = [sb.tile([P, V], F32, name="big%d" % t, align_bytes=64) for t in range(PACK)]
-
-        HS = S // 2
-        HV = V // 2
-        gate = [[sb.tile([P, HS], F32, name="gate%d_%d" % (h, t), align_bytes=64) for t in range(PACK)] for h in range(2)]
-        ctx_t = [sb.tile([P, PACK * HS], F32, name="ctx%d" % h, align_bytes=64) for h in range(2)]
-        part = [sb.tile([P, PACK * HV], F32, name="part%d" % h, align_bytes=64) for h in range(2)]
-        hid_bf = [sb.tile([P, PACK * HV], BF16, name="hid_bf%d" % h, align_bytes=64) for h in range(2)]
-        hid_q = [sb.tile([P, HV], U32, name="hid_q%d" % h, align_bytes=64) for h in range(2)]
-        hid_s = [sb.tile([P, HV], U8, name="hid_s%d" % h, align_bytes=64) for h in range(2)]
-        bind = [sb.tile([P, 4 * HV], F32, name="bind%d" % h, align_bytes=64) for h in range(2)]
+        mag = [tile("mag%d" % t, S, F32) for t in range(PACK)]
+        big = [tile("big%d" % t, V, F32) for t in range(PACK)]
+        gate = [[tile("gate%d_%d" % (h, t), HS, F32) for t in range(PACK)] for h in range(2)]
+        ctx_t = [tile("ctx%d" % h, PACK * HS, F32) for h in range(2)]
+        part = [tile("part%d" % h, PACK * HV, F32) for h in range(2)]
+        hid_bf = [tile("hid_bf%d" % h, PACK * HV, BF16) for h in range(2)]
+        hid_q = [tile("hid_q%d" % h, HV, U32) for h in range(2)]
+        hid_s = [tile("hid_s%d" % h, HV, U8) for h in range(2)]
+        bind = [tile("bind%d" % h, 4 * HV, F32) for h in range(2)]
 
         def magnitude(t):
             nc.scalar.activation(mag[t][:], ya[t][:], ACT.Abs)
@@ -187,9 +189,9 @@ def tile_picked_yhlaepi_esc_p_kernel(
             )
             nc.vector.quantize_mx(out=hid_q[h][:].bitcast(FP8X4), scales=hid_s[h][:], in_=hid_bf[h][:])
 
-        def score(h):
-            b = bank(h, "sc%d" % h)
+        def score(h, banks):
             for c in range(4):
+                b = banks[c]
                 nc.tensor.matmul_mx(
                     out=b[:, c * HV : (c + 1) * HV], lhsT=eg[:, c * P : (c + 1) * P].bitcast(FP8X4),
                     lhsT_scale=esg[:, c * P : (c + 1) * P], rhs=hid_q[h][:].bitcast(FP8X4), rhs_scale=hid_s[h][:],
@@ -197,15 +199,17 @@ def tile_picked_yhlaepi_esc_p_kernel(
                 )
             for c in range(4):
                 nc.scalar.activation(
-                    bind[h][:, c * HV : (c + 1) * HV], b[:, c * HV : (c + 1) * HV], ACT.Sigmoid,
+                    bind[h][:, c * HV : (c + 1) * HV], banks[c][:, c * HV : (c + 1) * HV], ACT.Sigmoid,
                     bias=thr_col[:, c : c + 1], scale=2.5,
                 )
 
+        eg = tile("eg", Z, U32, tag="w1_bf1")
         for t in range(PACK):
             magnitude(t)
             modulate(0, t)
             if t > 0:
                 join(0, t - 1)
+        nc.vector.tensor_copy(eg[:], ew[:].bitcast(U32).indirect(all_t[:]))
         modulate(1, 0)
         join(0, PACK - 1)
         modulate(1, 1)
@@ -216,23 +220,22 @@ def tile_picked_yhlaepi_esc_p_kernel(
         modulate(1, 3)
         join(1, 2)
         join(1, 3)
-        score(0)
+        score(0, [bank(0, "sc0")] * 4)
         quantise(1)
 
-        expr_ps = bank(2, "expr_ps")
+        expr_ps = bank(1, "expr_ps")
         for c in range(4):
-            nc.tensor.transpose(expr_ps[:, c * P : (c + 1) * P], te_col[:, c, 1:2].to_broadcast([P, P]), ident[:])
-        score(1)
+            nc.tensor.transpose(expr_ps[:, c * P : (c + 1) * P], te_col[:, 2 * c + 1 : 2 * c + 2].to_broadcast([P, P]), ident[:])
+        score(1, [bank(n, "sc1_%d" % n) for n in (2, 3, 6, 7)])
 
-        logs = sb.tile([P, 2 * Z], F32, name="logs", tag="thr_then_logs", align_bytes=64)
-        for h in range(2):
+        logs = tile("logs", 2 * Z, F32, tag="thr_then_logs")
+        for h, pieces in enumerate((((0, 512),), ((0, 384), (384, 512)))):
             turned = bank(4 + h, "turned%d" % h)
             for c in range(4):
                 nc.tensor.transpose(turned[:, c * P : (c + 1) * P], bind[h][:, c * HV : (c + 1) * HV], ident[:])
-            for half in range(2):
-                cols = slice(half * 256, (half + 1) * 256)
-                piece = logs[:, h * Z + half * 256 : h * Z + (half + 1) * 256]
-                res = sb.tile([P, 256], F32, name="res%d_%d" % (h, half), align_bytes=64)
-                nc.scalar.activation(piece, turned[:, cols], ACT.Ln, bias=1.1, scale=-0.8)
-                nc.vector.scalar_tensor_tensor(res[:], expr_ps[:, cols], 0.5, piece, ALU.mult, ALU.add)
-                nc.sync.dma_start(out=out[h * P : (h + 1) * P, cols], in_=res[:])
+            for a, b in pieces:
+                piece = logs[:, h * Z + a : h * Z + b]
+                res = tile("res%d_%d" % (h, a), b - a, F32)
+                nc.scalar.activation(piece, turned[:, a:b], ACT.Ln, bias=1.1, scale=-0.8)
+                nc.vector.scalar_tensor_tensor(res[:], expr_ps[:, a:b], 0.5, piece, ALU.mult, ALU.add)
+                nc.sync.dma_start(out=out[h * P : (h + 1) * P, a:b], in_=res[:])

@@ -45,7 +45,7 @@ def tile_picked_yhlaepi_esc_p_kernel(
         es = tile("es", T, U8)
         te = tile("te", T, F32)
         w2_raw = tile("w2_raw", PACK * H, F32)
-        w1_raw = tile("w1_raw", PACK * H, F32)
+        ew = tile("ew", T, I32)
         unit_t = tile("unit_t", PACK, F32)
         ident = tile("ident", P, F32)
 
@@ -65,8 +65,8 @@ def tile_picked_yhlaepi_esc_p_kernel(
         warm = tile("warm", 2, F32)
         nc.vector.memset(warm[:, 0:1], 0.0)
         nc.scalar.activation(warm[:, 1:2], warm[:, 0:1], ACT.Sigmoid)
-        nc.vector.memset(te[:, : T // 2], 0.0)
-        nc.gpsimd.memset(te[:, T // 2 :], 0.0)
+        nc.vector.memset(te[:, :896], 0.0)
+        nc.gpsimd.memset(te[:, 896:], 0.0)
         nc.vector.memset(es[:].bitcast(I32), 0)
         make_identity(nc, ident[:])
 
@@ -80,7 +80,7 @@ def tile_picked_yhlaepi_esc_p_kernel(
         load_words(xw, x_words)
         nc.sync.dma_start(out=unit_t[:], in_=unit.rearrange("(p t) o -> p (t o)", t=PACK))
         load_scales(nc.sync, es, e_scales)
-        load_weight(w1_raw, w1)
+        load_words(ew, e_words)
 
         def weight_tiles(name):
             return [
@@ -89,9 +89,9 @@ def tile_picked_yhlaepi_esc_p_kernel(
                 for u in range(2)
             ]
 
-        def deal(copy, tiles, raw, u):
+        def deal(copy, tiles, raw, u, m0=0, m1=P):
             copy(
-                tiles[u][0][:].rearrange("p (t m j) -> p m j t", t=2, j=PACK),
+                tiles[u][0][:].rearrange("p (t m j) -> p m j t", t=2, j=PACK)[:, m0:m1],
                 raw[:].rearrange("p (j m t) -> p m j t", t=PACK, j=PACK)[:, :, :, 2 * u : 2 * u + 2],
             )
 
@@ -107,14 +107,25 @@ def tile_picked_yhlaepi_esc_p_kernel(
         deal(nc.vector.tensor_copy, w2_t, w2_raw, 0)
         deal(nc.scalar.copy, w2_t, w2_raw, 1)
         nc.vector.tensor_copy(xsg[:], xs[:].indirect(offs_t[:]))
-        ew = tile("ew", T, I32, tag="w2_raw")
-        load_words(ew, e_words)
-        for u in range(2):
-            quantise_weight(w2_t, u)
+        w1_raw = [tile("w1_raw%d" % g, PACK * H // 2, F32, tag=tag) for g, tag in enumerate(("w2_raw", "xs"))]
+        for g in range(2):
+            nc.sync.dma_start(
+                out=w1_raw[g][:].rearrange("p (j c) -> p j c", j=PACK),
+                in_=w1.rearrange("(p j) c -> p j c", j=PACK)[:, :, g * (H // 2) : (g + 1) * (H // 2)],
+            )
+        quantise_weight(w2_t, 0)
         nc.vector.tensor_copy(xg[:], xw[:].bitcast(U32).indirect(offs_t[:]))
-        esg = tile("esg", Z, U8, tag="xw")
+        quantise_weight(w2_t, 1)
+        esg = tile("esg", Z, U8)
         nc.vector.tensor_copy(esg[:], es[:].indirect(all_t[:]))
+        eg = tile("eg", Z, U32)
+        nc.vector.tensor_copy(eg[:], ew[:].bitcast(U32).indirect(all_t[:]))
         nc.scalar.activation(teg[:], te[:].indirect(all_t[:]), ACT.Copy)
+
+        u8 = tile("u8", PACK, F32)
+        u3 = tile("u3", PACK, F32)
+        nc.scalar.activation(u8[:], unit_t[:], ACT.Copy, scale=0.8)
+        nc.scalar.activation(u3[:], unit_t[:], ACT.Copy, scale=0.3)
 
         def product(tiles, t, n, name):
             b = bank(n, "%s%d" % (name, t))
@@ -134,17 +145,15 @@ def tile_picked_yhlaepi_esc_p_kernel(
         sig = [tile("sig%d" % t, S, F32) for t in range(PACK)]
         for t in range(PACK):
             nc.scalar.activation(sig[t][:], ya[t][:], ACT.Sigmoid)
-        for u in range(2):
-            deal(nc.vector.tensor_copy, w1_t, w1_raw, u)
+        for g in range(2):
+            for u in range(2):
+                deal(nc.vector.tensor_copy, w1_t, w1_raw[g], u, g * (P // 2), (g + 1) * (P // 2))
 
-        te_col = tile("te_col", 8, F32)
+        te_rows = te_ps[:].rearrange("p (c r) -> p c r", r=P)
         thr_col = tile("thr_col", 4, F32, tag="thr_then_logs")
-        nc.scalar.copy(te_col[:].rearrange("p (c r) -> p c r", r=2), te_ps[:].rearrange("p (c r) -> p c r", r=P)[:, :, 0:2])
-        u8 = tile("u8", PACK, F32)
-        u3 = tile("u3", PACK, F32)
-        nc.gpsimd.tensor_scalar(u8[:], unit_t[:], 0.8, 0.0, ALU.mult, ALU.add)
-        nc.gpsimd.tensor_scalar(u3[:], unit_t[:], 0.3, 0.0, ALU.mult, ALU.add)
-        nc.gpsimd.tensor_scalar(thr_col[:], te_col[:, 0::2], -2.5, 0.0, ALU.mult, ALU.add)
+        expr_col = tile("expr_col", 4, F32)
+        nc.scalar.activation(thr_col[:], te_rows[:, :, 0], ACT.Copy, scale=-2.5)
+        nc.scalar.activation(expr_col[:], te_rows[:, :, 1], ACT.Copy)
 
         y = []
         for u in range(2):
@@ -152,7 +161,8 @@ def tile_picked_yhlaepi_esc_p_kernel(
             y.extend(product(w1_t, t, 4 + t, "y") for t in (2 * u, 2 * u + 1))
 
         mag = [tile("mag%d" % t, S, F32) for t in range(PACK)]
-        big = [tile("big%d" % t, V, F32) for t in range(PACK)]
+        bigs = [tile("big%d" % u, 2 * V, F32, tag="w1_bf%d" % u) for u in range(2)]
+        big = [bigs[t // 2][:, (t % 2) * V : (t % 2 + 1) * V] for t in range(PACK)]
         gate = [[tile("gate%d_%d" % (h, t), HS, F32) for t in range(PACK)] for h in range(2)]
         ctx_t = [tile("ctx%d" % h, PACK * HS, F32) for h in range(2)]
         part = [tile("part%d" % h, PACK * HV, F32) for h in range(2)]
@@ -163,7 +173,7 @@ def tile_picked_yhlaepi_esc_p_kernel(
 
         def magnitude(t):
             nc.scalar.activation(mag[t][:], ya[t][:], ACT.Abs)
-            nc.vector.tensor_tensor(big[t][:], mag[t][:, 0::2], mag[t][:, 1::2], ALU.max)
+            nc.vector.tensor_tensor(big[t], mag[t][:, 0::2], mag[t][:, 1::2], ALU.max)
 
         def modulate(h, t):
             nc.scalar.activation(
@@ -203,13 +213,11 @@ def tile_picked_yhlaepi_esc_p_kernel(
                     bias=thr_col[:, c : c + 1], scale=2.5,
                 )
 
-        eg = tile("eg", Z, U32, tag="w1_bf1")
         for t in range(PACK):
             magnitude(t)
             modulate(0, t)
             if t > 0:
                 join(0, t - 1)
-        nc.vector.tensor_copy(eg[:], ew[:].bitcast(U32).indirect(all_t[:]))
         modulate(1, 0)
         join(0, PACK - 1)
         modulate(1, 1)
@@ -225,7 +233,7 @@ def tile_picked_yhlaepi_esc_p_kernel(
 
         expr_ps = bank(1, "expr_ps")
         for c in range(4):
-            nc.tensor.transpose(expr_ps[:, c * P : (c + 1) * P], te_col[:, 2 * c + 1 : 2 * c + 2].to_broadcast([P, P]), ident[:])
+            nc.tensor.transpose(expr_ps[:, c * P : (c + 1) * P], expr_col[:, c : c + 1].to_broadcast([P, P]), ident[:])
         score(1, [bank(n, "sc1_%d" % n) for n in (2, 3, 6, 7)])
 
         logs = tile("logs", 2 * Z, F32, tag="thr_then_logs")

@@ -14,21 +14,34 @@ ACT = mybir.ActivationFunctionType
 ALU = mybir.AluOpType
 
 P = 128
-K, T, S, H, Z, V = 512, 2048, 512, 512, 512, 256
+K = 512
+T = 2048
+S = 512
+H = 512
+Z = 512
+V = 256
 PACK = 4
 HS = S // 2
 HV = V // 2
+CHUNKS = Z // P
+LIST_GROUP = 16
+LINE = 4
+
+CLEAR_SPLIT = 896
+OUT_PIECES = (((0, 128), (128, 512)), ((0, 384), (384, 512)))
+
 FLOPS = 2 * K * H * S * 2 + 2 * H * V * Z
+BYTES = 2 * K * T + 2 * (K // 32) * T + 2 * K * H * 4 + H * 4 + 2 * T * 4 + 3 * P * (S // LIST_GROUP) * 2 + V * Z * 4
 
 
 def tile_picked_yhlaepi_esc_p_kernel(
     tc, x_words, x_scales, w1, w2, e_words, e_scales, unit, thr, expr, offs, fl, all_, out
 ):
     nc = tc.nc
-    with ExitStack() as ctx:
-        lists = ctx.enter_context(tc.tile_pool(name="lists", bufs=1))
-        sb = ctx.enter_context(tc.tile_pool(name="sb", bufs=1))
-        psum = ctx.enter_context(tc.psum_pool(name="psum", bufs=1))
+    with ExitStack() as stack:
+        lists = stack.enter_context(tc.tile_pool(name="lists", bufs=1))
+        sb = stack.enter_context(tc.tile_pool(name="sb", bufs=1))
+        psum = stack.enter_context(tc.psum_pool(name="psum", bufs=1))
 
         def bank(n, name):
             return psum.tile([P, 512], F32, name=name, tag="bank%d" % n)
@@ -36,56 +49,56 @@ def tile_picked_yhlaepi_esc_p_kernel(
         def tile(name, columns, dtype, tag=None):
             return sb.tile([P, columns], dtype, name=name, tag=tag or name, align_bytes=64)
 
-        offs_t = lists.tile([P, S // 16], U16, name="offs_t")
-        fl_t = lists.tile([P, S // 16], U16, name="fl_t")
-        all_t = lists.tile([P, Z // 16], U16, name="all_t")
+        def half_of(list_tile, h):
+            return list_tile[:, h * (HS // LIST_GROUP) : (h + 1) * (HS // LIST_GROUP)]
 
-        xw = tile("xw", T, I32)
-        xs = tile("xs", T, U8)
-        es = tile("es", T, U8)
-        te = tile("te", T, F32)
+        offs_t = lists.tile([P, S // LIST_GROUP], U16, name="offs_t")
+        fl_t = lists.tile([P, S // LIST_GROUP], U16, name="fl_t")
+        all_t = lists.tile([P, Z // LIST_GROUP], U16, name="all_t")
+
+        x_table = tile("x_table", T, I32)
+        x_scale_table = tile("x_scale_table", T, U8)
+        e_scale_table = tile("e_scale_table", T, U8)
+        row_table = tile("row_table", T, F32)
         w2_raw = tile("w2_raw", PACK * H, F32)
-        ew = tile("ew", T, I32)
+        e_table = tile("e_table", T, I32)
         unit_t = tile("unit_t", PACK, F32)
         ident = tile("ident", P, F32)
 
-        def load_scales(queue, dst, scales):
+        def load_scales(dst, scales):
             for q in range(4):
-                queue.dma_start(
+                nc.sync.dma_start(
                     out=dst[32 * q : 32 * q + 4, :].bitcast(I32), in_=scales[0][4 * q : 4 * q + 4, :].bitcast(I32)
                 )
 
         def load_words(dst, words):
             nc.sync.dma_start(out=dst[:], in_=words[0].rearrange("p n t -> p (n t)").bitcast(I32))
 
-        def load_weight(dst, w):
-            nc.sync.dma_start(out=dst[:], in_=w.rearrange("(p j) c -> p (j c)", j=PACK))
-
-        nc.gpsimd.memset(xs[:].bitcast(I32), 0)
-        warm = tile("warm", 2, F32)
-        nc.vector.memset(warm[:, 0:1], 0.0)
-        nc.scalar.activation(warm[:, 1:2], warm[:, 0:1], ACT.Sigmoid)
-        nc.vector.memset(te[:, :896], 0.0)
-        nc.gpsimd.memset(te[:, 896:], 0.0)
-        nc.vector.memset(es[:].bitcast(I32), 0)
+        nc.gpsimd.memset(x_scale_table[:].bitcast(I32), 0)
+        nc.vector.memset(row_table[:, :CLEAR_SPLIT], 0.0)
+        nc.gpsimd.memset(row_table[:, CLEAR_SPLIT:], 0.0)
+        nc.vector.memset(e_scale_table[:].bitcast(I32), 0)
         make_identity(nc, ident[:])
 
         nc.sync.dma_start(offs_t[:], offs)
         nc.sync.dma_start(all_t[:], all_)
         nc.sync.dma_start(fl_t[:], fl)
-        load_weight(w2_raw, w2)
-        load_scales(nc.sync, xs, x_scales)
-        nc.sync.dma_start(out=te[0:1, :], in_=thr[0:1, :])
-        nc.sync.dma_start(out=te[1:2, :], in_=expr[0:1, :])
-        load_words(xw, x_words)
+        nc.sync.dma_start(out=w2_raw[:], in_=w2.rearrange("(p j) c -> p (j c)", j=PACK))
+        load_scales(x_scale_table, x_scales)
+        nc.sync.dma_start(out=row_table[0:1, :], in_=thr[0:1, :])
+        nc.sync.dma_start(out=row_table[1:2, :], in_=expr[0:1, :])
+        load_words(x_table, x_words)
         nc.sync.dma_start(out=unit_t[:], in_=unit.rearrange("(p t) o -> p (t o)", t=PACK))
-        load_scales(nc.sync, es, e_scales)
-        load_words(ew, e_words)
+        load_scales(e_scale_table, e_scales)
+        load_words(e_table, e_words)
 
         def weight_tiles(name):
             return [
-                (tile("%s_bf%d" % (name, u), 2 * P * PACK, BF16), tile("%s_q%d" % (name, u), 2 * P, U32),
-                 tile("%s_s%d" % (name, u), 2 * P, U8))
+                (
+                    tile("%s_bf%d" % (name, u), 2 * P * PACK, BF16),
+                    tile("%s_q%d" % (name, u), 2 * P, U32),
+                    tile("%s_s%d" % (name, u), 2 * P, U8),
+                )
                 for u in range(2)
             ]
 
@@ -98,152 +111,192 @@ def tile_picked_yhlaepi_esc_p_kernel(
         def quantise_weight(tiles, u):
             nc.vector.quantize_mx(out=tiles[u][1][:].bitcast(FP8X4), scales=tiles[u][2][:], in_=tiles[u][0][:])
 
-        xsg = tile("xsg", S, U8)
-        xg = tile("xg", S, U32)
-        teg = tile("teg", Z, F32)
+        x_scale_picked = tile("x_scale_picked", S, U8)
+        x_picked = [tile("x_picked%d" % h, HS, U32) for h in range(2)]
+        rows_picked = tile("rows_picked", Z, F32)
         w2_t = weight_tiles("w2")
         w1_t = weight_tiles("w1")
 
         deal(nc.vector.tensor_copy, w2_t, w2_raw, 0)
         deal(nc.scalar.copy, w2_t, w2_raw, 1)
-        nc.vector.tensor_copy(xsg[:], xs[:].indirect(offs_t[:]))
-        w1_raw = [tile("w1_raw%d" % g, PACK * H // 2, F32, tag=tag) for g, tag in enumerate(("w2_raw", "xs"))]
+        nc.vector.tensor_copy(x_scale_picked[:], x_scale_table[:].indirect(offs_t[:]))
+
+        w1_raw = [
+            tile("w1_raw%d" % g, PACK * H // 2, F32, tag=tag) for g, tag in enumerate(("w2_raw", "x_scale_table"))
+        ]
         for g in range(2):
             nc.sync.dma_start(
                 out=w1_raw[g][:].rearrange("p (j c) -> p j c", j=PACK),
                 in_=w1.rearrange("(p j) c -> p j c", j=PACK)[:, :, g * (H // 2) : (g + 1) * (H // 2)],
             )
-        quantise_weight(w2_t, 0)
-        nc.vector.tensor_copy(xg[:], xw[:].bitcast(U32).indirect(offs_t[:]))
-        quantise_weight(w2_t, 1)
-        esg = tile("esg", Z, U8)
-        nc.vector.tensor_copy(esg[:], es[:].indirect(all_t[:]))
-        eg = tile("eg", Z, U32)
-        nc.vector.tensor_copy(eg[:], ew[:].bitcast(U32).indirect(all_t[:]))
-        nc.scalar.activation(teg[:], te[:].indirect(all_t[:]), ACT.Copy)
 
-        u8 = tile("u8", PACK, F32)
-        u3 = tile("u3", PACK, F32)
-        nc.scalar.activation(u8[:], unit_t[:], ACT.Copy, scale=0.8)
-        nc.scalar.activation(u3[:], unit_t[:], ACT.Copy, scale=0.3)
+        for n in range(2):
+            quantise_weight(w2_t, n)
+            nc.vector.tensor_copy(x_picked[n][:], x_table[:].bitcast(U32).indirect(half_of(offs_t, n)))
+        e_scale_picked = tile("e_scale_picked", Z, U8)
+        nc.vector.tensor_copy(e_scale_picked[:], e_scale_table[:].indirect(all_t[:]))
+        e_picked = tile("e_picked", Z, U32)
+        nc.vector.tensor_copy(e_picked[:], e_table[:].bitcast(U32).indirect(all_t[:]))
+        nc.scalar.activation(rows_picked[:], row_table[:].indirect(all_t[:]), ACT.Copy)
 
-        def product(tiles, t, n, name):
-            b = bank(n, "%s%d" % (name, t))
+        unit_gate = tile("unit_gate", PACK, F32)
+        unit_mag = tile("unit_mag", PACK, F32)
+        nc.gpsimd.tensor_scalar(unit_gate[:], unit_t[:], 0.8, 0.0, ALU.mult, ALU.add)
+        nc.gpsimd.tensor_scalar(unit_mag[:], unit_t[:], 0.3, 0.0, ALU.mult, ALU.add)
+
+        def product(dst, tiles, t, h):
             cols = slice((t % 2) * P, (t % 2 + 1) * P)
             nc.tensor.matmul_mx(
-                out=b[:], lhsT=tiles[t // 2][1][:, cols].bitcast(FP8X4), lhsT_scale=tiles[t // 2][2][:, cols],
-                rhs=xg[:].bitcast(FP8X4), rhs_scale=xsg[:], start=True, stop=True,
+                out=dst,
+                lhsT=tiles[t // 2][1][:, cols].bitcast(FP8X4),
+                lhsT_scale=tiles[t // 2][2][:, cols],
+                rhs=x_picked[h][:].bitcast(FP8X4),
+                rhs_scale=x_scale_picked[:, h * HS : (h + 1) * HS],
+                start=True,
+                stop=True,
             )
-            return b
 
-        ya = [product(w2_t, t, t, "ya") for t in range(PACK)]
+        ya = [[bank(2 * h + u, "ya%d_%d" % (h, u)) for u in range(2)] for h in range(2)]
+        sig = [tile("sig%d" % u, 2 * S, F32) for u in range(2)]
+        for h in range(2):
+            for u in range(2):
+                for i in range(2):
+                    product(ya[h][u][:, i * HS : (i + 1) * HS], w2_t, 2 * u + i, h)
+                nc.scalar.activation(
+                    sig[u][:].rearrange("p (i s) -> p i s", i=2)[:, :, h * HS : (h + 1) * HS],
+                    ya[h][u][:].rearrange("p (i s) -> p i s", i=2),
+                    ACT.Sigmoid,
+                )
 
-        te_ps = bank(7, "te_ps")
-        for c in range(4):
-            nc.tensor.transpose(te_ps[:, c * P : (c + 1) * P], teg[:, c * P : (c + 1) * P], ident[:])
-
-        sig = [tile("sig%d" % t, S, F32) for t in range(PACK)]
-        for t in range(PACK):
-            nc.scalar.activation(sig[t][:], ya[t][:], ACT.Sigmoid)
         for g in range(2):
             for u in range(2):
                 deal(nc.vector.tensor_copy, w1_t, w1_raw[g], u, g * (P // 2), (g + 1) * (P // 2))
 
-        te_rows = te_ps[:].rearrange("p (c r) -> p c r", r=P)
-        thr_col = tile("thr_col", 4, F32, tag="thr_then_logs")
-        expr_col = tile("expr_col", 4, F32)
-        nc.scalar.activation(thr_col[:], te_rows[:, :, 0], ACT.Copy, scale=-2.5)
-        nc.scalar.activation(expr_col[:], te_rows[:, :, 1], ACT.Copy)
-
-        y = []
+        y = [bank(4 + t, "y%d" % t) for t in range(PACK)]
         for u in range(2):
             quantise_weight(w1_t, u)
-            y.extend(product(w1_t, t, 4 + t, "y") for t in (2 * u, 2 * u + 1))
+            for t in (2 * u, 2 * u + 1):
+                for h in range(2):
+                    product(y[t][:, h * HS : (h + 1) * HS], w1_t, t, h)
 
-        mag = [tile("mag%d" % t, S, F32) for t in range(PACK)]
-        bigs = [tile("big%d" % u, 2 * V, F32, tag="w1_bf%d" % u) for u in range(2)]
-        big = [bigs[t // 2][:, (t % 2) * V : (t % 2 + 1) * V] for t in range(PACK)]
+        mag = [[tile("mag%d_%d" % (h, u), 2 * HS, F32) for u in range(2)] for h in range(2)]
         gate = [[tile("gate%d_%d" % (h, t), HS, F32) for t in range(PACK)] for h in range(2)]
-        ctx_t = [tile("ctx%d" % h, PACK * HS, F32) for h in range(2)]
+        gated = [tile("gated%d" % h, PACK * HS, F32) for h in range(2)]
         part = [tile("part%d" % h, PACK * HV, F32) for h in range(2)]
         hid_bf = [tile("hid_bf%d" % h, PACK * HV, BF16) for h in range(2)]
         hid_q = [tile("hid_q%d" % h, HV, U32) for h in range(2)]
         hid_s = [tile("hid_s%d" % h, HV, U8) for h in range(2)]
-        bind = [tile("bind%d" % h, 4 * HV, F32) for h in range(2)]
+        bind = [tile("bind%d" % h, CHUNKS * HV, F32) for h in range(2)]
 
-        def magnitude(t):
-            nc.scalar.activation(mag[t][:], ya[t][:], ACT.Abs)
-            nc.vector.tensor_tensor(big[t], mag[t][:, 0::2], mag[t][:, 1::2], ALU.max)
+        def magnitude(h, u):
+            nc.scalar.activation(mag[h][u][:], ya[h][u][:], ACT.Abs)
+            nc.vector.tensor_tensor(
+                larger[h][:, 2 * u * HV : 2 * (u + 1) * HV], mag[h][u][:, 0::2], mag[h][u][:, 1::2], ALU.max
+            )
 
         def modulate(h, t):
-            nc.scalar.activation(
-                gate[h][t][:], sig[t][:].indirect(fl_t[:, h * (HS // 16) : (h + 1) * (HS // 16)]), ACT.Copy, bias=0.5
-            )
+            window = sig[t // 2][:, (t % 2) * S : (t % 2 + 1) * S]
+            nc.scalar.activation(gate[h][t][:], window.indirect(half_of(fl_t, h)), ACT.Copy, bias=0.5)
             nc.vector.scalar_tensor_tensor(
-                ctx_t[h][:, t * HS : (t + 1) * HS], gate[h][t][:], u8[:, t : t + 1], y[t][:, h * HS : (h + 1) * HS],
-                ALU.mult, ALU.mult,
+                gated[h][:, t * HS : (t + 1) * HS],
+                gate[h][t][:],
+                unit_gate[:, t : t + 1],
+                y[t][:, h * HS : (h + 1) * HS],
+                ALU.mult,
+                ALU.mult,
             )
 
         def join(h, t):
             nc.vector.scalar_tensor_tensor(
-                part[h][:, t * HV : (t + 1) * HV], big[t][:, h * HV : (h + 1) * HV], u3[:, t : t + 1],
-                ctx_t[h][:, t * HS : (t + 1) * HS : 2], ALU.mult, ALU.add,
+                part[h][:, t * HV : (t + 1) * HV],
+                larger[h][:, t * HV : (t + 1) * HV],
+                unit_mag[:, t : t + 1],
+                gated[h][:, t * HS : (t + 1) * HS : 2],
+                ALU.mult,
+                ALU.add,
             )
 
-        def quantise(h):
+        def quantise_hid(h):
             nc.vector.tensor_tensor(
-                hid_bf[h][:].rearrange("p (c i t) -> p c t i", i=4, t=PACK),
-                part[h][:].rearrange("p (t c i) -> p c t i", i=4, t=PACK),
-                ctx_t[h][:].rearrange("p (t c i d) -> p c t i d", i=4, t=PACK, d=2)[:, :, :, :, 1],
+                hid_bf[h][:].rearrange("p (c i t) -> p c t i", i=LINE, t=PACK),
+                part[h][:].rearrange("p (t c i) -> p c t i", i=LINE, t=PACK),
+                gated[h][:].rearrange("p (t c i d) -> p c t i d", i=LINE, t=PACK, d=2)[:, :, :, :, 1],
                 ALU.add,
             )
             nc.vector.quantize_mx(out=hid_q[h][:].bitcast(FP8X4), scales=hid_s[h][:], in_=hid_bf[h][:])
 
         def score(h, banks):
-            for c in range(4):
-                b = banks[c]
+            for c in range(CHUNKS):
                 nc.tensor.matmul_mx(
-                    out=b[:, c * HV : (c + 1) * HV], lhsT=eg[:, c * P : (c + 1) * P].bitcast(FP8X4),
-                    lhsT_scale=esg[:, c * P : (c + 1) * P], rhs=hid_q[h][:].bitcast(FP8X4), rhs_scale=hid_s[h][:],
-                    start=True, stop=True,
+                    out=banks[c][:, c * HV : (c + 1) * HV],
+                    lhsT=e_picked[:, c * P : (c + 1) * P].bitcast(FP8X4),
+                    lhsT_scale=e_scale_picked[:, c * P : (c + 1) * P],
+                    rhs=hid_q[h][:].bitcast(FP8X4),
+                    rhs_scale=hid_s[h][:],
+                    start=True,
+                    stop=True,
                 )
-            for c in range(4):
+            for c in range(CHUNKS):
                 nc.scalar.activation(
-                    bind[h][:, c * HV : (c + 1) * HV], banks[c][:, c * HV : (c + 1) * HV], ACT.Sigmoid,
-                    bias=thr_col[:, c : c + 1], scale=2.5,
+                    bind[h][:, c * HV : (c + 1) * HV],
+                    banks[c][:, c * HV : (c + 1) * HV],
+                    ACT.Sigmoid,
+                    bias=thr_col[:, c : c + 1],
+                    scale=2.5,
                 )
 
-        for t in range(PACK):
-            magnitude(t)
-            modulate(0, t)
-            if t > 0:
-                join(0, t - 1)
+        larger = [tile("larger0", PACK * HV, F32, tag="w1_bf1")]
+        magnitude(0, 0)
+
+        rows_turned = bank(0, "rows_turned")
+        for c in range(CHUNKS):
+            nc.tensor.transpose(rows_turned[:, c * P : (c + 1) * P], rows_picked[:, c * P : (c + 1) * P], ident[:])
+
+        modulate(0, 0)
+        modulate(0, 1)
+        join(0, 0)
+        magnitude(0, 1)
+        join(0, 1)
+        rows_by_chunk = rows_turned[:].rearrange("p (c r) -> p c r", r=P)
+        thr_col = tile("thr_col", CHUNKS, F32, tag="thr_then_logs")
+        expr_col = tile("expr_col", CHUNKS, F32)
+        nc.scalar.activation(thr_col[:], rows_by_chunk[:, :, 0], ACT.Copy, scale=-2.5)
+        nc.scalar.activation(expr_col[:], rows_by_chunk[:, :, 1], ACT.Copy)
+
+        modulate(0, 2)
+        modulate(0, 3)
+        join(0, 2)
+        join(0, 3)
         modulate(1, 0)
-        join(0, PACK - 1)
+        quantise_hid(0)
+        larger.append(tile("larger1", PACK * HV, F32, tag="part0"))
+        magnitude(1, 0)
         modulate(1, 1)
-        quantise(0)
         join(1, 0)
-        modulate(1, 2)
+        magnitude(1, 1)
         join(1, 1)
+        modulate(1, 2)
         modulate(1, 3)
         join(1, 2)
         join(1, 3)
-        score(0, [bank(0, "sc0")] * 4)
-        quantise(1)
+        score(0, [bank(0, "score0")] * CHUNKS)
+        quantise_hid(1)
 
-        expr_ps = bank(1, "expr_ps")
-        for c in range(4):
-            nc.tensor.transpose(expr_ps[:, c * P : (c + 1) * P], expr_col[:, c : c + 1].to_broadcast([P, P]), ident[:])
-        score(1, [bank(n, "sc1_%d" % n) for n in (2, 3, 6, 7)])
+        expr_spread = bank(4, "expr_spread")
+        for c in range(CHUNKS):
+            nc.tensor.transpose(
+                expr_spread[:, c * P : (c + 1) * P], expr_col[:, c : c + 1].to_broadcast([P, P]), ident[:]
+            )
+        score(1, [bank(n, "score1_%d" % n) for n in (2, 3, 6, 7)])
 
         logs = tile("logs", 2 * Z, F32, tag="thr_then_logs")
-        for h, pieces in enumerate((((0, 512),), ((0, 384), (384, 512)))):
-            turned = bank(4 + h, "turned%d" % h)
-            for c in range(4):
-                nc.tensor.transpose(turned[:, c * P : (c + 1) * P], bind[h][:, c * HV : (c + 1) * HV], ident[:])
-            for a, b in pieces:
+        for h, free_bank in enumerate((1, 5)):
+            bind_turned = bank(free_bank, "bind_turned%d" % h)
+            for c in range(CHUNKS):
+                nc.tensor.transpose(bind_turned[:, c * P : (c + 1) * P], bind[h][:, c * HV : (c + 1) * HV], ident[:])
+            for a, b in OUT_PIECES[h]:
                 piece = logs[:, h * Z + a : h * Z + b]
                 res = tile("res%d_%d" % (h, a), b - a, F32)
-                nc.scalar.activation(piece, turned[:, a:b], ACT.Ln, bias=1.1, scale=-0.8)
-                nc.vector.scalar_tensor_tensor(res[:], expr_ps[:, a:b], 0.5, piece, ALU.mult, ALU.add)
+                nc.scalar.activation(piece, bind_turned[:, a:b], ACT.Ln, bias=1.1, scale=-0.8)
+                nc.vector.scalar_tensor_tensor(res[:], expr_spread[:, a:b], 0.5, piece, ALU.mult, ALU.add)
                 nc.sync.dma_start(out=out[h * P : (h + 1) * P, a:b], in_=res[:])

from contextlib import ExitStack

import concourse.mybir as mybir
from concourse.masks import make_identity

F32 = mybir.dt.float32
BF16 = mybir.dt.bfloat16
I32 = mybir.dt.int32
U32 = mybir.dt.uint32
U16 = mybir.dt.uint16
U8 = mybir.dt.uint8
FP8X4 = mybir.dt.float8_e4m3fn_x4
ACT = mybir.ActivationFunctionType
ALU = mybir.AluOpType

P = 128
K = 512
T = 2048
S = 512
H = 512
Z = 512
V = 256
PACK = 4
HS = S // 2
HV = V // 2
CHUNKS = Z // P
LIST_GROUP = 16
LINE = 4

CLEAR_SPLIT = 896
OUT_PIECES = (((0, 128), (128, 512)), ((0, 384), (384, 512)))

FLOPS = 2 * K * H * S * 2 + 2 * H * V * Z
BYTES = 2 * K * T + 2 * (K // 32) * T + 2 * K * H * 4 + H * 4 + 2 * T * 4 + 3 * P * (S // LIST_GROUP) * 2 + V * Z * 4


def tile_picked_yhlaepi_esc_p_kernel(
    tc, x_words, x_scales, w1, w2, e_words, e_scales, unit, thr, expr, offs, fl, all_, out
):
    nc = tc.nc
    with ExitStack() as stack:
        lists = stack.enter_context(tc.tile_pool(name="lists", bufs=1))
        sb = stack.enter_context(tc.tile_pool(name="sb", bufs=1))
        psum = stack.enter_context(tc.psum_pool(name="psum", bufs=1))

        def bank(n, name):
            return psum.tile([P, 512], F32, name=name, tag="bank%d" % n)

        def tile(name, columns, dtype, tag=None):
            return sb.tile([P, columns], dtype, name=name, tag=tag or name, align_bytes=64)

        def half_of(list_tile, h):
            return list_tile[:, h * (HS // LIST_GROUP) : (h + 1) * (HS // LIST_GROUP)]

        offs_t = lists.tile([P, S // LIST_GROUP], U16, name="offs_t")
        fl_t = lists.tile([P, S // LIST_GROUP], U16, name="fl_t")
        all_t = lists.tile([P, Z // LIST_GROUP], U16, name="all_t")

        x_table = tile("x_table", T, I32)
        x_scale_table = tile("x_scale_table", T, U8)
        e_scale_table = tile("e_scale_table", T, U8)
        row_table = tile("row_table", T, F32)
        w2_raw = tile("w2_raw", PACK * H, F32)
        e_table = tile("e_table", T, I32)
        unit_t = tile("unit_t", PACK, F32)
        ident = tile("ident", P, F32)

        def load_scales(dst, scales):
            for q in range(4):
                nc.sync.dma_start(
                    out=dst[32 * q : 32 * q + 4, :].bitcast(I32), in_=scales[0][4 * q : 4 * q + 4, :].bitcast(I32)
                )

        def load_words(dst, words):
            nc.sync.dma_start(out=dst[:], in_=words[0].rearrange("p n t -> p (n t)").bitcast(I32))

        nc.gpsimd.memset(x_scale_table[:].bitcast(I32), 0)
        nc.vector.memset(row_table[:, :CLEAR_SPLIT], 0.0)
        nc.gpsimd.memset(row_table[:, CLEAR_SPLIT:], 0.0)
        nc.vector.memset(e_scale_table[:].bitcast(I32), 0)
        make_identity(nc, ident[:])

        nc.sync.dma_start(offs_t[:], offs)
        nc.sync.dma_start(all_t[:], all_)
        nc.sync.dma_start(fl_t[:], fl)
        nc.sync.dma_start(out=w2_raw[:], in_=w2.rearrange("(p j) c -> p (j c)", j=PACK))
        load_scales(x_scale_table, x_scales)
        nc.sync.dma_start(out=row_table[0:1, :], in_=thr[0:1, :])
        nc.sync.dma_start(out=row_table[1:2, :], in_=expr[0:1, :])
        load_words(x_table, x_words)
        nc.sync.dma_start(out=unit_t[:], in_=unit.rearrange("(p t) o -> p (t o)", t=PACK))
        load_scales(e_scale_table, e_scales)
        load_words(e_table, e_words)

        def weight_tiles(name):
            return [
                (
                    tile("%s_bf%d" % (name, u), 2 * P * PACK, BF16),
                    tile("%s_q%d" % (name, u), 2 * P, U32),
                    tile("%s_s%d" % (name, u), 2 * P, U8),
                )
                for u in range(2)
            ]

        def deal(copy, tiles, raw, u, m0=0, m1=P):
            copy(
                tiles[u][0][:].rearrange("p (t m j) -> p m j t", t=2, j=PACK)[:, m0:m1],
                raw[:].rearrange("p (j m t) -> p m j t", t=PACK, j=PACK)[:, :, :, 2 * u : 2 * u + 2],
            )

        def quantise_weight(tiles, u):
            nc.vector.quantize_mx(out=tiles[u][1][:].bitcast(FP8X4), scales=tiles[u][2][:], in_=tiles[u][0][:])

        x_scale_picked = tile("x_scale_picked", S, U8)
        x_picked = [tile("x_picked%d" % h, HS, U32) for h in range(2)]
        rows_picked = tile("rows_picked", Z, F32)
        w2_t = weight_tiles("w2")
        w1_t = weight_tiles("w1")

        deal(nc.vector.tensor_copy, w2_t, w2_raw, 0)
        deal(nc.scalar.copy, w2_t, w2_raw, 1)
        nc.vector.tensor_copy(x_scale_picked[:], x_scale_table[:].indirect(offs_t[:]))

        w1_raw = [
            tile("w1_raw%d" % g, PACK * H // 2, F32, tag=tag) for g, tag in enumerate(("w2_raw", "x_scale_table"))
        ]
        for g in range(2):
            nc.sync.dma_start(
                out=w1_raw[g][:].rearrange("p (j c) -> p j c", j=PACK),
                in_=w1.rearrange("(p j) c -> p j c", j=PACK)[:, :, g * (H // 2) : (g + 1) * (H // 2)],
            )

        for n in range(2):
            quantise_weight(w2_t, n)
            nc.vector.tensor_copy(x_picked[n][:], x_table[:].bitcast(U32).indirect(half_of(offs_t, n)))
        e_scale_picked = tile("e_scale_picked", Z, U8)
        nc.vector.tensor_copy(e_scale_picked[:], e_scale_table[:].indirect(all_t[:]))
        e_picked = tile("e_picked", Z, U32)
        nc.vector.tensor_copy(e_picked[:], e_table[:].bitcast(U32).indirect(all_t[:]))
        nc.scalar.activation(rows_picked[:], row_table[:].indirect(all_t[:]), ACT.Copy)

        unit_gate = tile("unit_gate", PACK, F32)
        unit_mag = tile("unit_mag", PACK, F32)
        nc.gpsimd.tensor_scalar(unit_gate[:], unit_t[:], 0.8, 0.0, ALU.mult, ALU.add)
        nc.gpsimd.tensor_scalar(unit_mag[:], unit_t[:], 0.3, 0.0, ALU.mult, ALU.add)

        def product(dst, tiles, t, h):
            cols = slice((t % 2) * P, (t % 2 + 1) * P)
            nc.tensor.matmul_mx(
                out=dst,
                lhsT=tiles[t // 2][1][:, cols].bitcast(FP8X4),
                lhsT_scale=tiles[t // 2][2][:, cols],
                rhs=x_picked[h][:].bitcast(FP8X4),
                rhs_scale=x_scale_picked[:, h * HS : (h + 1) * HS],
                start=True,
                stop=True,
            )

        ya = [[bank(2 * h + u, "ya%d_%d" % (h, u)) for u in range(2)] for h in range(2)]
        sig = [tile("sig%d" % u, 2 * S, F32) for u in range(2)]
        for h in range(2):
            for u in range(2):
                for i in range(2):
                    product(ya[h][u][:, i * HS : (i + 1) * HS], w2_t, 2 * u + i, h)
                nc.scalar.activation(
                    sig[u][:].rearrange("p (i s) -> p i s", i=2)[:, :, h * HS : (h + 1) * HS],
                    ya[h][u][:].rearrange("p (i s) -> p i s", i=2),
                    ACT.Sigmoid,
                )

        for g in range(2):
            for u in range(2):
                deal(nc.vector.tensor_copy, w1_t, w1_raw[g], u, g * (P // 2), (g + 1) * (P // 2))

        y = [bank(4 + t, "y%d" % t) for t in range(PACK)]
        for u in range(2):
            quantise_weight(w1_t, u)
            for t in (2 * u, 2 * u + 1):
                for h in range(2):
                    product(y[t][:, h * HS : (h + 1) * HS], w1_t, t, h)

        mag = [[tile("mag%d_%d" % (h, u), 2 * HS, F32) for u in range(2)] for h in range(2)]
        gate = [[tile("gate%d_%d" % (h, t), HS, F32) for t in range(PACK)] for h in range(2)]
        gated = [tile("gated%d" % h, PACK * HS, F32) for h in range(2)]
        part = [tile("part%d" % h, PACK * HV, F32) for h in range(2)]
        hid_bf = [tile("hid_bf%d" % h, PACK * HV, BF16) for h in range(2)]
        hid_q = [tile("hid_q%d" % h, HV, U32) for h in range(2)]
        hid_s = [tile("hid_s%d" % h, HV, U8) for h in range(2)]
        bind = [tile("bind%d" % h, CHUNKS * HV, F32) for h in range(2)]

        def magnitude(h, u):
            nc.scalar.activation(mag[h][u][:], ya[h][u][:], ACT.Abs)
            nc.vector.tensor_tensor(
                larger[h][:, 2 * u * HV : 2 * (u + 1) * HV], mag[h][u][:, 0::2], mag[h][u][:, 1::2], ALU.max
            )

        def modulate(h, t):
            window = sig[t // 2][:, (t % 2) * S : (t % 2 + 1) * S]
            nc.scalar.activation(gate[h][t][:], window.indirect(half_of(fl_t, h)), ACT.Copy, bias=0.5)
            nc.vector.scalar_tensor_tensor(
                gated[h][:, t * HS : (t + 1) * HS],
                gate[h][t][:],
                unit_gate[:, t : t + 1],
                y[t][:, h * HS : (h + 1) * HS],
                ALU.mult,
                ALU.mult,
            )

        def join(h, t):
            nc.vector.scalar_tensor_tensor(
                part[h][:, t * HV : (t + 1) * HV],
                larger[h][:, t * HV : (t + 1) * HV],
                unit_mag[:, t : t + 1],
                gated[h][:, t * HS : (t + 1) * HS : 2],
                ALU.mult,
                ALU.add,
            )

        def quantise_hid(h):
            nc.vector.tensor_tensor(
                hid_bf[h][:].rearrange("p (c i t) -> p c t i", i=LINE, t=PACK),
                part[h][:].rearrange("p (t c i) -> p c t i", i=LINE, t=PACK),
                gated[h][:].rearrange("p (t c i d) -> p c t i d", i=LINE, t=PACK, d=2)[:, :, :, :, 1],
                ALU.add,
            )
            nc.vector.quantize_mx(out=hid_q[h][:].bitcast(FP8X4), scales=hid_s[h][:], in_=hid_bf[h][:])

        def score(h, banks):
            for c in range(CHUNKS):
                nc.tensor.matmul_mx(
                    out=banks[c][:, c * HV : (c + 1) * HV],
                    lhsT=e_picked[:, c * P : (c + 1) * P].bitcast(FP8X4),
                    lhsT_scale=e_scale_picked[:, c * P : (c + 1) * P],
                    rhs=hid_q[h][:].bitcast(FP8X4),
                    rhs_scale=hid_s[h][:],
                    start=True,
                    stop=True,
                )
            for c in range(CHUNKS):
                nc.scalar.activation(
                    bind[h][:, c * HV : (c + 1) * HV],
                    banks[c][:, c * HV : (c + 1) * HV],
                    ACT.Sigmoid,
                    bias=thr_col[:, c : c + 1],
                    scale=2.5,
                )

        larger = [tile("larger0", PACK * HV, F32, tag="w1_bf1")]
        magnitude(0, 0)

        rows_turned = bank(0, "rows_turned")
        for c in range(CHUNKS):
            nc.tensor.transpose(rows_turned[:, c * P : (c + 1) * P], rows_picked[:, c * P : (c + 1) * P], ident[:])

        modulate(0, 0)
        modulate(0, 1)
        join(0, 0)
        magnitude(0, 1)
        join(0, 1)
        rows_by_chunk = rows_turned[:].rearrange("p (c r) -> p c r", r=P)
        thr_col = tile("thr_col", CHUNKS, F32, tag="thr_then_logs")
        expr_col = tile("expr_col", CHUNKS, F32)
        nc.scalar.activation(thr_col[:], rows_by_chunk[:, :, 0], ACT.Copy, scale=-2.5)
        nc.scalar.activation(expr_col[:], rows_by_chunk[:, :, 1], ACT.Copy)

        modulate(0, 2)
        modulate(0, 3)
        join(0, 2)
        join(0, 3)
        modulate(1, 0)
        quantise_hid(0)
        larger.append(tile("larger1", PACK * HV, F32, tag="part0"))
        magnitude(1, 0)
        modulate(1, 1)
        join(1, 0)
        magnitude(1, 1)
        join(1, 1)
        modulate(1, 2)
        modulate(1, 3)
        join(1, 2)
        join(1, 3)
        score(0, [bank(0, "score0")] * CHUNKS)
        quantise_hid(1)

        expr_spread = bank(4, "expr_spread")
        for c in range(CHUNKS):
            nc.tensor.transpose(
                expr_spread[:, c * P : (c + 1) * P], expr_col[:, c : c + 1].to_broadcast([P, P]), ident[:]
            )
        score(1, [bank(n, "score1_%d" % n) for n in (2, 3, 6, 7)])

        logs = tile("logs", 2 * Z, F32, tag="thr_then_logs")
        for h, free_bank in enumerate((1, 5)):
            bind_turned = bank(free_bank, "bind_turned%d" % h)
            for c in range(CHUNKS):
                nc.tensor.transpose(bind_turned[:, c * P : (c + 1) * P], bind[h][:, c * HV : (c + 1) * HV], ident[:])
            for a, b in OUT_PIECES[h]:
                piece = logs[:, h * Z + a : h * Z + b]
                res = tile("res%d_%d" % (h, a), b - a, F32)
                nc.scalar.activation(piece, bind_turned[:, a:b], ACT.Ln, bias=1.1, scale=-0.8)
                nc.vector.scalar_tensor_tensor(res[:], expr_spread[:, a:b], 0.5, piece, ALU.mult, ALU.add)
                nc.sync.dma_start(out=out[h * P : (h + 1) * P, a:b], in_=res[:])
